import numpy as np
import ml_dtypes


def mxq(x, axis, fmt="e4m3"):
    dtype, down = {"e4m3": (ml_dtypes.float8_e4m3fn, 7), "e5m2": (ml_dtypes.float8_e5m2, 14)}[fmt]
    v = np.moveaxis(np.asarray(x, np.float32).astype(ml_dtypes.bfloat16).astype(np.float64), axis, -1)
    blocks = v.reshape(v.shape[:-1] + (-1, 32))
    amax = np.abs(blocks).max(-1, keepdims=True)
    byte = np.maximum(np.where(amax > 0, np.frexp(amax)[1] - 1 + 127, 0) - down, 1)
    scale = np.exp2(byte - 127.0)
    codes = (blocks / scale).astype(np.float32).astype(dtype).astype(np.float64)
    return np.moveaxis((codes * scale).reshape(v.shape), -1, axis)


WIDE = False


def mx_kscale(k):
    if not WIDE:
        return np.ones(k)
    levels = np.array([10, -10, 5, -5, 0])
    if k % 512:
        return np.exp2(np.random.permutation(np.resize(levels, k // 32))).repeat(32)
    a = np.empty((k // 512, 16))
    for p in range(k // 512):
        a[p, :8] = np.random.permutation(np.resize(levels, 8))
        for g in range(8):
            far = levels[np.abs(levels - a[p, g]) >= 10]
            a[p, g + 8] = far[np.random.randint(len(far))]
    return np.exp2(a.ravel()).repeat(32)


def f64(x):
    return np.asarray(x).astype(np.float64)


def striped(idx):
    return np.tile(idx.reshape(-1, 16).T, (8, 1)).astype(np.uint16)


def unstriped(offs):
    return offs[:16].T.reshape(-1).astype(np.int64)


def striped8(idx):
    return np.concatenate([x.reshape(-1, 16).T for x in idx]).astype(np.uint16)


def runs(offs, k):
    lists = np.stack([offs[16 * r : 16 * r + 16].T.reshape(-1) for r in range(8)]).astype(np.int64)
    return lists[np.arange(k) % 512 // 64]


def pack_weight(w):
    k, n = w.shape
    w = f64(np.asarray(w, np.float32).astype(ml_dtypes.bfloat16)).reshape(k // 32, 32, n)
    amax = np.abs(w).max(1)
    byte = np.clip(np.where(amax > 0, np.frexp(amax)[1] - 1 + 127 - 7, 1), 1, 254)
    scaled = (w * np.exp2(127.0 - byte)[:, None, :]).reshape(k, n).astype(np.float32)
    words = np.ascontiguousarray(scaled.reshape(k // 512, 128, 4, n).transpose(0, 1, 3, 2)).astype(ml_dtypes.float8_e4m3fn).view(np.uint8)
    return words, np.ascontiguousarray(byte.astype(np.uint8).reshape(k // 512, 16, n))


def unpack_weight(words, scales):
    g, p, n, _ = words.shape
    vals = np.ascontiguousarray(words).view(ml_dtypes.float8_e4m3fn).astype(np.float64) * np.repeat(np.exp2(scales.astype(np.float64) - 127.0), 8, axis=1)[..., None]
    return vals.transpose(0, 1, 3, 2).reshape(g * 512, n)


def sigmoid(v):
    return 1.0 / (1.0 + np.exp(-np.maximum(v, -700.0)))


K, T, S, N, G, H, W, U = 512, 2048, 512, 512, 2048, 512, 1024, 384


def setup_inputs():
    n = np.random.standard_normal
    s = mx_kscale(K)[:, None]
    u = mx_kscale(S)
    packed_xT = pack_weight(n((K, T)) * s)
    packed_dT = pack_weight(n((K, G)) / s)
    return {
        "x_words": packed_xT[0],
        "x_scales": packed_xT[1],
        "d_words": packed_dT[0],
        "d_scales": packed_dT[1],
        "gn": (np.random.uniform(0.5, 1.5, (H, 1)) * u[:, None]).astype(np.float32),
        "w1": (n((H, N)) / np.sqrt(H) / u[:, None]).astype(np.float32),
        "offs": striped8(np.random.randint(0, T, (8, S))),
        "k1": striped8(np.random.randint(0, G, (8, H))),
        "n1": striped(np.random.randint(0, S, W)),
        "n2": striped(np.random.permutation(S)),
        "n3": striped(np.random.permutation(S)[:U]),
        "n4": striped(np.random.permutation(S)[:U]),
    }


def reference(x_words, x_scales, d_words, d_scales, gn, w1, offs, k1, n1, n2, n3, n4):
    d_k1 = unpack_weight(d_words, d_scales)[np.arange(K)[:, None], runs(k1, K)]
    xq = unpack_weight(x_words, x_scales)[np.arange(K)[:, None], runs(offs, K)]
    h = 0.0625 * (d_k1.T @ xq)
    mb = h[:, unstriped(n1)]
    mx = mb.reshape(H, S, 2).max(axis=2)
    st = h - mx
    z = f64(gn) * (np.maximum(st, st[:, unstriped(n2)]))
    h2 = mxq(f64(w1), 0, "e4m3").T @ mxq(z, 0, "e4m3")
    old = h2[:, unstriped(n3)]
    pa = h2[:, unstriped(n4)]
    ra = old * sigmoid(pa)
    out = h2.copy()
    out[:, unstriped(n3)] = ra
    return out

@@ -1,0 +1,238 @@
+from contextlib import ExitStack
+
+import concourse.mybir as mybir
+
+F32 = mybir.dt.float32
+BF16 = mybir.dt.bfloat16
+I32 = mybir.dt.int32
+U32 = mybir.dt.uint32
+U16 = mybir.dt.uint16
+U8 = mybir.dt.uint8
+FP8X4 = mybir.dt.float8_e4m3fn_x4
+ALU = mybir.AluOpType
+ACT = mybir.ActivationFunctionType
+
+P = 128
+PACK = 4
+T = 2048
+S = 512
+U = 384
+FLOPS = 2 * 2 * 512 * 512 * 512
+
+H_WINDOW = 520
+ST_WINDOW = 688
+H2_WINDOW = 768
+
+
+def gather(nc, engine, out, window, offsets):
+    if engine == "vector":
+        nc.vector.tensor_copy(out=out, in_=window.indirect(offsets))
+    else:
+        nc.scalar.activation(out=out, in_=window.indirect(offsets), func=ACT.Copy)
+
+
+def tile_picked_hpqghopmkgate_none_p_kernel(
+    tc, x_words, x_scales, d_words, d_scales, gn, w1, offs, k1, n1, n2, n3, n4, out
+):
+    nc = tc.nc
+    with ExitStack() as ctx:
+        lists = ctx.enter_context(tc.tile_pool(name="lists", bufs=1))
+        sb = ctx.enter_context(tc.tile_pool(name="sb", bufs=1))
+        psum = ctx.enter_context(tc.psum_pool(name="psum", bufs=1))
+
+        def load_list(src, name):
+            dst = lists.tile(list(src.shape), U16, name=name)
+            nc.sync.dma_start(out=dst[:], in_=src)
+            return dst
+
+        def load_scale_table(src, name, memset_engine):
+            dst = sb.tile([P, T], U8, name=name, align_bytes=64)
+            nc.sync.dma_start(out=dst[:].bitcast(I32), in_=src[0].bitcast(I32).unsqueeze(1).to_broadcast([16, 8, T // 4]))
+            return dst
+
+        def load_word_table(src, name):
+            dst = sb.tile([P, T], I32, name=name, tag=name, align_bytes=64)
+            nc.sync.dma_start(out=dst[:], in_=src[0].rearrange("p n t -> p (n t)").bitcast(I32))
+            return dst
+
+        k1_sb = load_list(k1, "k1_sb")
+        d_scale_table = load_scale_table(d_scales, "d_scale_table", nc.vector)
+        offs_sb = load_list(offs, "offs_sb")
+        x_scale_table = load_scale_table(x_scales, "x_scale_table", nc.gpsimd)
+        d_word_table = load_word_table(d_words, "d_word_table")
+        x_word_table = load_word_table(x_words, "x_word_table")
+        n1_sb = load_list(n1, "n1_sb")
+        n2_sb = load_list(n2, "n2_sb")
+        n3_sb = load_list(n3, "n3_sb")
+        n4_sb = load_list(n4, "n4_sb")
+
+        h = [sb.tile([P, H_WINDOW], F32, name="h%d" % t) for t in range(PACK)]
+        st = [sb.tile([P, ST_WINDOW], F32, name="st%d" % t) for t in range(PACK)]
+        h2 = [sb.tile([P, H2_WINDOW], F32, name="h2_%d" % t) for t in range(PACK)]
+        for window in h + st + h2:
+            nc.gpsimd.memset(window[:, S:], 0.0)
+
+        d_bytes = sb.tile([P, S], U8, name="d_bytes", tag="d_bytes", align_bytes=64)
+        nc.vector.tensor_copy(out=d_bytes[:], in_=d_scale_table[:].indirect(k1_sb[:]))
+        d_plane = sb.tile([P, S], U8, name="d_plane", align_bytes=64)
+        nc.vector.tensor_copy(
+            out=d_plane[:].rearrange("p (t m) -> p m t", t=PACK), in_=d_bytes[:].rearrange("p (m t) -> p m t", t=PACK)
+        )
+        for j in range(1, 4):
+            nc.scalar.dma_start(out=d_plane[j:P:32, :].bitcast(I32), in_=d_plane[8 * j : P : 32, :].bitcast(I32))
+        x_bytes = sb.tile([P, S], U8, name="x_bytes", align_bytes=64)
+        nc.vector.tensor_copy(out=x_bytes[:], in_=x_scale_table[:].indirect(offs_sb[:]))
+        x_plane = sb.tile([P, S], U8, name="x_plane", align_bytes=64)
+        nc.gpsimd.memset(x_plane[:], 0)
+        for j in range(4):
+            nc.scalar.dma_start(out=x_plane[j:P:32, :].bitcast(I32), in_=x_bytes[8 * j : P : 32, :].bitcast(I32))
+
+        gn_sb = sb.tile([P, PACK], F32, name="gn_sb", tag="d_bytes", align_bytes=64)
+        nc.sync.dma_start(out=gn_sb[:], in_=gn.rearrange("(p t) o -> p (t o)", t=PACK))
+
+        d_picked = sb.tile([P, S], I32, name="d_picked", align_bytes=64)
+        nc.vector.tensor_copy(out=d_picked[:].bitcast(U32), in_=d_word_table[:].bitcast(U32).indirect(k1_sb[:]))
+        d_dealt = sb.tile([P, S], I32, name="d_dealt", align_bytes=64)
+        nc.vector.tensor_copy(
+            out=d_dealt[:].rearrange("p (t a i) -> p a t i", t=PACK, i=4),
+            in_=d_picked[:].rearrange("p (a i t) -> p a t i", t=PACK, i=4),
+        )
+        x_picked = sb.tile([P, S], I32, name="x_picked", align_bytes=64)
+        nc.vector.tensor_copy(out=x_picked[:].bitcast(U32), in_=x_word_table[:].bitcast(U32).indirect(offs_sb[:]))
+
+        w_raw = sb.tile([P, PACK, S], F32, name="w_raw", tag="x_word_table", align_bytes=64)
+        nc.sync.dma_start(out=w_raw[:], in_=w1.rearrange("(p t) m -> p t m", t=PACK))
+
+        h_ps = [psum.tile([P, S], F32, name="h_ps%d" % t) for t in range(PACK)]
+        for t in range(PACK):
+            nc.tensor.matmul_mx(
+                out=h_ps[t][:],
+                lhsT=d_dealt[:, P * t : P * (t + 1)].bitcast(FP8X4),
+                lhsT_scale=d_plane[:, P * t : P * (t + 1)],
+                rhs=x_picked[:].bitcast(FP8X4),
+                rhs_scale=x_plane[:],
+                start=True,
+                stop=True,
+            )
+
+        members = [sb.tile([P, 2 * S], F32, name="members%d" % t, tag="members%d" % t, align_bytes=64) for t in range(PACK)]
+        z_pairs_all = sb.tile([P, 2, S, 2], BF16, name="z_pairs", align_bytes=64)
+
+        def leave_psum(t):
+            nc.scalar.activation(out=h[t][:, :S], in_=h_ps[t][:], func=ACT.Copy, scale=0.0625)
+
+        def fetch_members(t, engine):
+            for half in range(2):
+                gather(nc, engine, members[t][:, S * half : S * (half + 1)], h[t][:], n1_sb[:, 32 * half : 32 * (half + 1)])
+
+        def make_st(t, parts=1):
+            mx = sb.tile([P, S], F32, name="mx%d" % t)
+            n = S // parts
+            for i in range(parts):
+                lo, hi = n * i, n * (i + 1)
+                nc.vector.tensor_tensor(
+                    out=mx[:, lo:hi], in0=members[t][:, 2 * lo : 2 * hi : 2], in1=members[t][:, 2 * lo + 1 : 2 * hi : 2], op=ALU.max
+                )
+                nc.vector.tensor_tensor(out=st[t][:, lo:hi], in0=h[t][:, lo:hi], in1=mx[:, lo:hi], op=ALU.subtract)
+
+        other = [sb.tile([P, S], F32, name="other%d" % t) for t in range(PACK)]
+
+        def fetch_other(t, engine):
+            gather(nc, engine, other[t][:], st[t][:], n2_sb[:])
+
+        def make_z(t):
+            larger = sb.tile([P, S], F32, name="larger%d" % t)
+            nc.vector.tensor_tensor(out=larger[:], in0=st[t][:, :S], in1=other[t][:], op=ALU.max)
+            nc.vector.tensor_scalar(
+                out=z_pairs_all[:, t // 2, :, t % 2], in0=larger[:], scalar1=gn_sb[:, t : t + 1], scalar2=None, op0=ALU.mult
+            )
+
+        leave_psum(0)
+        leave_psum(1)
+        fetch_members(0, "vector")
+        fetch_members(1, "scalar")
+        make_st(0)
+        leave_psum(2)
+        fetch_members(2, "scalar")
+        make_st(1)
+        fetch_other(0, "vector")
+        make_z(0)
+        leave_psum(3)
+        fetch_members(3, "scalar")
+        make_st(2)
+        make_st(3, parts=2)
+        fetch_other(1, "scalar")
+        fetch_other(2, "scalar")
+        fetch_other(3, "vector")
+        make_z(1)
+        make_z(3)
+        make_z(2)
+
+        w_codes = sb.tile([P, S], I32, name="w_codes", align_bytes=64)
+        w_scales = sb.tile([P, S], U8, name="w_scales", align_bytes=64)
+        for half in range(2):
+            cols = slice(256 * half, 256 * (half + 1))
+            w_grouped = sb.tile([P, 256 * PACK], BF16, name="w_grouped%d" % half, tag="members%d" % (2 + half), align_bytes=64)
+            nc.scalar.copy(
+                out=w_grouped[:].rearrange("p (c i t) -> p c t i", t=PACK, i=4),
+                in_=w_raw[:, :, cols].rearrange("p t (c i) -> p c t i", i=4),
+            )
+            nc.vector.quantize_mx(out=w_codes[:, cols].bitcast(FP8X4), scales=w_scales[:, cols], in_=w_grouped[:])
+
+        z_grouped = sb.tile([P, S * PACK], BF16, name="z_grouped", align_bytes=64)
+        z_words = z_grouped[:].bitcast(I32).rearrange("p (c e) -> p c e", e=2)
+        nc.vector.tensor_copy(out=z_words, in_=z_pairs_all[:].rearrange("p e c b -> p (e c b)").bitcast(I32).rearrange("p (e c) -> p c e", e=2))
+        z_codes = sb.tile([P, S], I32, name="z_codes", align_bytes=64)
+        z_scales = sb.tile([P, S], U8, name="z_scales", align_bytes=64)
+        nc.vector.quantize_mx(out=z_codes[:].bitcast(FP8X4), scales=z_scales[:], in_=z_grouped[:])
+
+        h2_ps = [psum.tile([P, S], F32, name="h2_ps%d" % u) for u in range(PACK)]
+        for u in range(PACK):
+            nc.tensor.matmul_mx(
+                out=h2_ps[u][:],
+                lhsT=w_codes[:, P * u : P * (u + 1)].bitcast(FP8X4),
+                lhsT_scale=w_scales[:, P * u : P * (u + 1)],
+                rhs=z_codes[:].bitcast(FP8X4),
+                rhs_scale=z_scales[:],
+                start=True,
+                stop=True,
+            )
+
+        def gate(u):
+            g = sb.tile([P, U], F32, name="gate%d" % u)
+            nc.scalar.activation(out=g[:], in_=h2[u][:].indirect(n4_sb[:]), func=ACT.Sigmoid)
+            return g
+
+        def store(u):
+            nc.sync.dma_start(out=out[P * u : P * (u + 1), :], in_=h2[u][:, :S])
+
+        def scatter_on_scalar(u, g):
+            ra = sb.tile([P, U], F32, name="ra%d" % u)
+            nc.vector.tensor_tensor(out=ra[:], in0=h2[u][:].indirect(n3_sb[:]), in1=g[:], op=ALU.mult)
+            return lambda: nc.scalar.activation(out=h2[u][:].indirect(n3_sb[:]), in_=ra[:], func=ACT.Copy)
+
+        def scatter_on_vector(u):
+            old = sb.tile([P, U], F32, name="old%d" % u)
+            nc.vector.tensor_copy(out=old[:], in_=h2[u][:].indirect(n3_sb[:]))
+            return lambda g: nc.vector.tensor_tensor(out=h2[u][:].indirect(n3_sb[:]), in0=old[:], in1=g[:], op=ALU.mult)
+
+        nc.vector.tensor_copy(out=h2[0][:, :S], in_=h2_ps[0][:])
+        gate0 = gate(0)
+        nc.vector.tensor_copy(out=h2[1][:, :S], in_=h2_ps[1][:])
+        nc.scalar.copy(out=h2[2][:, :S], in_=h2_ps[2][:])
+        put1 = scatter_on_vector(1)
+        gate2 = gate(2)
+        put0 = scatter_on_scalar(0, gate0)
+        gate1 = gate(1)
+        put2 = scatter_on_scalar(2, gate2)
+        put0()
+        store(0)
+        put1(gate1)
+        store(1)
+        nc.scalar.copy(out=h2[3][:, :S], in_=h2_ps[3][:])
+        gate3 = gate(3)
+        put3 = scatter_on_vector(3)
+        put2()
+        store(2)
+        put3(gate3)
+        store(3)

@@ -46,8 +46,9 @@ def tile_picked_hpqghopmkgate_none_p_kernel(
             return dst
 
         def load_scale_table(src, name, memset_engine):
-            dst = sb.tile([P, T], U8, name=name, align_bytes=64)
-            nc.sync.dma_start(out=dst[:].bitcast(I32), in_=src[0].bitcast(I32).unsqueeze(1).to_broadcast([16, 8, T // 4]))
+            dst = sb.tile([P, T], U8, name=name, tag=name, align_bytes=64)
+            memset_engine.memset(dst[:].bitcast(I32), 0)
+            nc.sync.dma_start(out=dst[0:P:8, :].bitcast(I32), in_=src[0].bitcast(I32))
             return dst
 
         def load_word_table(src, name):
@@ -56,9 +57,9 @@ def tile_picked_hpqghopmkgate_none_p_kernel(
             return dst
 
         k1_sb = load_list(k1, "k1_sb")
-        d_scale_table = load_scale_table(d_scales, "d_scale_table", nc.vector)
         offs_sb = load_list(offs, "offs_sb")
-        x_scale_table = load_scale_table(x_scales, "x_scale_table", nc.gpsimd)
+        d_scale_table = load_scale_table(d_scales, "d_scale_table", nc.gpsimd)
+        x_scale_table = load_scale_table(x_scales, "x_scale_table", nc.vector)
         d_word_table = load_word_table(d_words, "d_word_table")
         x_word_table = load_word_table(x_words, "x_word_table")
         n1_sb = load_list(n1, "n1_sb")
@@ -72,51 +73,81 @@ def tile_picked_hpqghopmkgate_none_p_kernel(
         for window in h + st + h2:
             nc.gpsimd.memset(window[:, S:], 0.0)
 
+        warm = sb.tile([P, 1], F32, name="warm")
+        nc.scalar.activation(out=warm[:], in_=h[0][:, S : S + 1], func=ACT.Sigmoid)
+
         d_bytes = sb.tile([P, S], U8, name="d_bytes", tag="d_bytes", align_bytes=64)
         nc.vector.tensor_copy(out=d_bytes[:], in_=d_scale_table[:].indirect(k1_sb[:]))
-        d_plane = sb.tile([P, S], U8, name="d_plane", align_bytes=64)
-        nc.vector.tensor_copy(
-            out=d_plane[:].rearrange("p (t m) -> p m t", t=PACK), in_=d_bytes[:].rearrange("p (m t) -> p m t", t=PACK)
-        )
-        for j in range(1, 4):
-            nc.scalar.dma_start(out=d_plane[j:P:32, :].bitcast(I32), in_=d_plane[8 * j : P : 32, :].bitcast(I32))
-        x_bytes = sb.tile([P, S], U8, name="x_bytes", align_bytes=64)
+        x_bytes = sb.tile([P, S], U8, name="x_bytes", tag="x_bytes", align_bytes=64)
         nc.vector.tensor_copy(out=x_bytes[:], in_=x_scale_table[:].indirect(offs_sb[:]))
-        x_plane = sb.tile([P, S], U8, name="x_plane", align_bytes=64)
-        nc.gpsimd.memset(x_plane[:], 0)
-        for j in range(4):
-            nc.scalar.dma_start(out=x_plane[j:P:32, :].bitcast(I32), in_=x_bytes[8 * j : P : 32, :].bitcast(I32))
+        planes = sb.tile([P, 2 * S], U8, name="planes", tag="x_scale_table", align_bytes=64)
+        nc.vector.tensor_copy(
+            out=planes[:, S:].rearrange("p (t m) -> p t m", t=PACK), in_=d_bytes[:].rearrange("p (m t) -> p t m", t=PACK)
+        )
+        nc.vector.tensor_copy(out=planes[:, :S].bitcast(I32), in_=x_bytes[:].bitcast(I32))
+        for j in range(1, 4):
+            nc.scalar.dma_start(out=planes[j:P:32, :].bitcast(I32), in_=planes[8 * j : P : 32, :].bitcast(I32))
+
+        halves = [slice(0, S // 2), slice(S // 2, S)]
+        w_rows = w1.rearrange("(p t) m -> p t m", t=PACK)
+        w_raw0 = sb.tile([P, PACK, S // 2], F32, name="w_raw0", tag="x_bytes", align_bytes=64)
+        nc.scalar.dma_start(out=w_raw0[:], in_=w_rows[:, :, halves[0]])
 
         gn_sb = sb.tile([P, PACK], F32, name="gn_sb", tag="d_bytes", align_bytes=64)
         nc.sync.dma_start(out=gn_sb[:], in_=gn.rearrange("(p t) o -> p (t o)", t=PACK))
 
         d_picked = sb.tile([P, S], I32, name="d_picked", align_bytes=64)
-        nc.vector.tensor_copy(out=d_picked[:].bitcast(U32), in_=d_word_table[:].bitcast(U32).indirect(k1_sb[:]))
+        for c in halves:
+            nc.vector.tensor_copy(
+                out=d_picked[:, c].bitcast(U32), in_=d_word_table[:].bitcast(U32).indirect(k1_sb[:, c.start // 16 : c.stop // 16])
+            )
         d_dealt = sb.tile([P, S], I32, name="d_dealt", align_bytes=64)
-        nc.vector.tensor_copy(
-            out=d_dealt[:].rearrange("p (t a i) -> p a t i", t=PACK, i=4),
-            in_=d_picked[:].rearrange("p (a i t) -> p a t i", t=PACK, i=4),
-        )
+        for c in halves:
+            nc.vector.tensor_copy(
+                out=d_dealt[:].rearrange("p (t a i) -> p a t i", t=PACK, i=4)[:, c.start // 16 : c.stop // 16],
+                in_=d_picked[:, c].rearrange("p (a i t) -> p a t i", t=PACK, i=4),
+            )
         x_picked = sb.tile([P, S], I32, name="x_picked", align_bytes=64)
-        nc.vector.tensor_copy(out=x_picked[:].bitcast(U32), in_=x_word_table[:].bitcast(U32).indirect(offs_sb[:]))
+        for c in halves:
+            nc.vector.tensor_copy(
+                out=x_picked[:, c].bitcast(U32), in_=x_word_table[:].bitcast(U32).indirect(offs_sb[:, c.start // 16 : c.stop // 16])
+            )
 
-        w_raw = sb.tile([P, PACK, S], F32, name="w_raw", tag="x_word_table", align_bytes=64)
-        nc.sync.dma_start(out=w_raw[:], in_=w1.rearrange("(p t) m -> p t m", t=PACK))
+        w_raw1 = sb.tile([P, PACK, S // 2], F32, name="w_raw1", tag="x_word_table", align_bytes=64)
+        nc.sync.dma_start(out=w_raw1[:], in_=w_rows[:, :, halves[1]])
 
-        h_ps = [psum.tile([P, S], F32, name="h_ps%d" % t) for t in range(PACK)]
-        for t in range(PACK):
+        def quantize_w(raw, copy, grouped_tag, codes_tag):
+            w_grouped = sb.tile([P, 256 * PACK], BF16, name="w_grouped", tag=grouped_tag, align_bytes=64)
+            copy(
+                out=w_grouped[:].rearrange("p (c i t) -> p c t i", t=PACK, i=4),
+                in_=raw[:].rearrange("p t (c i) -> p c t i", i=4),
+            )
+            codes = sb.tile([P, S // 2], I32, name="w_codes", tag=codes_tag, align_bytes=64)
+            scales = sb.tile([P, S // 2], U8, name="w_scales", tag=codes_tag + "_scales", align_bytes=64)
+            nc.vector.quantize_mx(out=codes[:].bitcast(FP8X4), scales=scales[:], in_=w_grouped[:])
+            return codes, scales
+
+        def product(dst, lhs_codes, lhs_scales, t, rhs_codes, rhs_scales, c):
+            rows = slice(P * t, P * (t + 1))
             nc.tensor.matmul_mx(
-                out=h_ps[t][:],
-                lhsT=d_dealt[:, P * t : P * (t + 1)].bitcast(FP8X4),
-                lhsT_scale=d_plane[:, P * t : P * (t + 1)],
-                rhs=x_picked[:].bitcast(FP8X4),
-                rhs_scale=x_plane[:],
+                out=dst,
+                lhsT=lhs_codes[:, rows].bitcast(FP8X4),
+                lhsT_scale=lhs_scales[:, rows],
+                rhs=rhs_codes[:, c].bitcast(FP8X4),
+                rhs_scale=rhs_scales[:, c],
                 start=True,
                 stop=True,
             )
 
+        h_ps = [psum.tile([P, S], F32, name="h_ps%d" % t, tag="bank%d" % t) for t in range(PACK)]
+        for t in range(PACK):
+            for c in halves if t == 0 else [slice(0, S)]:
+                product(h_ps[t][:, c], d_dealt, planes[:, S:], t, x_picked, planes[:, :S], c)
+        w_codes0, w_scales0 = quantize_w(w_raw0, nc.vector.tensor_copy, "w_grouped0", "w_codes0")
+
         members = [sb.tile([P, 2 * S], F32, name="members%d" % t, tag="members%d" % t, align_bytes=64) for t in range(PACK)]
-        z_pairs_all = sb.tile([P, 2, S, 2], BF16, name="z_pairs", align_bytes=64)
+        z_both = [sb.tile([P, 2 * S], BF16, name="z_both%d" % i, align_bytes=64) for i in range(2)]
+        z_pairs = [[z_both[i][:, S * e : S * (e + 1)] for e in range(2)] for i in range(2)]
 
         def leave_psum(t):
             nc.scalar.activation(out=h[t][:, :S], in_=h_ps[t][:], func=ACT.Copy, scale=0.0625)
@@ -125,78 +156,74 @@ def tile_picked_hpqghopmkgate_none_p_kernel(
             for half in range(2):
                 gather(nc, engine, members[t][:, S * half : S * (half + 1)], h[t][:], n1_sb[:, 32 * half : 32 * (half + 1)])
 
-        def make_st(t, parts=1):
-            mx = sb.tile([P, S], F32, name="mx%d" % t)
-            n = S // parts
-            for i in range(parts):
-                lo, hi = n * i, n * (i + 1)
+        def make_st(t):
+            mx = sb.tile([P, S], F32, name="mx%d" % t, tag="mx%d" % t, align_bytes=64)
+            for c in halves:
                 nc.vector.tensor_tensor(
-                    out=mx[:, lo:hi], in0=members[t][:, 2 * lo : 2 * hi : 2], in1=members[t][:, 2 * lo + 1 : 2 * hi : 2], op=ALU.max
+                    out=mx[:, c],
+                    in0=members[t][:, 2 * c.start : 2 * c.stop : 2],
+                    in1=members[t][:, 2 * c.start + 1 : 2 * c.stop : 2],
+                    op=ALU.max,
                 )
-                nc.vector.tensor_tensor(out=st[t][:, lo:hi], in0=h[t][:, lo:hi], in1=mx[:, lo:hi], op=ALU.subtract)
+            for c in halves:
+                nc.vector.tensor_tensor(out=st[t][:, c], in0=h[t][:, c], in1=mx[:, c], op=ALU.subtract)
 
         other = [sb.tile([P, S], F32, name="other%d" % t) for t in range(PACK)]
 
-        def fetch_other(t, engine):
-            gather(nc, engine, other[t][:], st[t][:], n2_sb[:])
+        def fetch_other(t, *engines):
+            n = S // len(engines)
+            for i, engine in enumerate(engines):
+                gather(nc, engine, other[t][:, n * i : n * (i + 1)], st[t][:], n2_sb[:, n * i // 16 : n * (i + 1) // 16])
 
         def make_z(t):
             larger = sb.tile([P, S], F32, name="larger%d" % t)
-            nc.vector.tensor_tensor(out=larger[:], in0=st[t][:, :S], in1=other[t][:], op=ALU.max)
-            nc.vector.tensor_scalar(
-                out=z_pairs_all[:, t // 2, :, t % 2], in0=larger[:], scalar1=gn_sb[:, t : t + 1], scalar2=None, op0=ALU.mult
-            )
+            for c in halves:
+                nc.vector.tensor_tensor(out=larger[:, c], in0=st[t][:, c], in1=other[t][:, c], op=ALU.max)
+            for i, c in enumerate(halves):
+                nc.vector.tensor_scalar(
+                    out=z_pairs[i][t // 2][:, t % 2 : S : 2], in0=larger[:, c], scalar1=gn_sb[:, t : t + 1], scalar2=None, op0=ALU.mult
+                )
 
         leave_psum(0)
         leave_psum(1)
+        leave_psum(2)
         fetch_members(0, "vector")
         fetch_members(1, "scalar")
         make_st(0)
-        leave_psum(2)
+        leave_psum(3)
         fetch_members(2, "scalar")
         make_st(1)
-        fetch_other(0, "vector")
+        fetch_other(0, "vector", "vector")
         make_z(0)
-        leave_psum(3)
         fetch_members(3, "scalar")
         make_st(2)
-        make_st(3, parts=2)
-        fetch_other(1, "scalar")
-        fetch_other(2, "scalar")
-        fetch_other(3, "vector")
+        fetch_other(1, "scalar", "scalar")
+        make_st(3)
         make_z(1)
-        make_z(3)
+        fetch_other(2, "scalar", "scalar")
+        fetch_other(3, "scalar", "scalar")
         make_z(2)
+        make_z(3)
 
-        w_codes = sb.tile([P, S], I32, name="w_codes", align_bytes=64)
-        w_scales = sb.tile([P, S], U8, name="w_scales", align_bytes=64)
-        for half in range(2):
-            cols = slice(256 * half, 256 * (half + 1))
-            w_grouped = sb.tile([P, 256 * PACK], BF16, name="w_grouped%d" % half, tag="members%d" % (2 + half), align_bytes=64)
-            nc.scalar.copy(
-                out=w_grouped[:].rearrange("p (c i t) -> p c t i", t=PACK, i=4),
-                in_=w_raw[:, :, cols].rearrange("p t (c i) -> p c t i", i=4),
-            )
-            nc.vector.quantize_mx(out=w_codes[:, cols].bitcast(FP8X4), scales=w_scales[:, cols], in_=w_grouped[:])
-
-        z_grouped = sb.tile([P, S * PACK], BF16, name="z_grouped", align_bytes=64)
-        z_words = z_grouped[:].bitcast(I32).rearrange("p (c e) -> p c e", e=2)
-        nc.vector.tensor_copy(out=z_words, in_=z_pairs_all[:].rearrange("p e c b -> p (e c b)").bitcast(I32).rearrange("p (e c) -> p c e", e=2))
         z_codes = sb.tile([P, S], I32, name="z_codes", align_bytes=64)
         z_scales = sb.tile([P, S], U8, name="z_scales", align_bytes=64)
-        nc.vector.quantize_mx(out=z_codes[:].bitcast(FP8X4), scales=z_scales[:], in_=z_grouped[:])
-
-        h2_ps = [psum.tile([P, S], F32, name="h2_ps%d" % u) for u in range(PACK)]
-        for u in range(PACK):
-            nc.tensor.matmul_mx(
-                out=h2_ps[u][:],
-                lhsT=w_codes[:, P * u : P * (u + 1)].bitcast(FP8X4),
-                lhsT_scale=w_scales[:, P * u : P * (u + 1)],
-                rhs=z_codes[:].bitcast(FP8X4),
-                rhs_scale=z_scales[:],
-                start=True,
-                stop=True,
+        z_grouped = [sb.tile([P, S * 2], BF16, name="z_grouped%d" % i, tag="z_grouped%d" % i, align_bytes=64) for i in range(2)]
+        for i in range(2):
+            nc.vector.tensor_copy(
+                out=z_grouped[i][:].bitcast(I32).rearrange("p (c e) -> p c e", e=2),
+                in_=z_both[i][:].bitcast(I32).rearrange("p (e c) -> p c e", e=2),
             )
+        for i, c in enumerate(halves):
+            nc.vector.quantize_mx(out=z_codes[:, c].bitcast(FP8X4), scales=z_scales[:, c], in_=z_grouped[i][:])
+        w_codes1, w_scales1 = quantize_w(w_raw1, nc.scalar.copy, "mx3", "z_grouped1")
+
+        early = [[psum.tile([P, S // 2], F32, name="early%d%d" % (u, i), tag="bank%d" % (4 + 2 * u + i)) for i in range(2)] for u in range(2)]
+        late = [psum.tile([P, S], F32, name="late%d" % u, tag="bank%d" % u) for u in range(2)]
+        for i, c in enumerate(halves):
+            for u in range(2):
+                product(early[u][i][:], w_codes0, w_scales0, u, z_codes, z_scales, c)
+        for u in range(2):
+            product(late[u][:], w_codes1, w_scales1, u, z_codes, z_scales, slice(0, S))
 
         def gate(u):
             g = sb.tile([P, U], F32, name="gate%d" % u)
@@ -211,28 +238,30 @@ def tile_picked_hpqghopmkgate_none_p_kernel(
             nc.vector.tensor_tensor(out=ra[:], in0=h2[u][:].indirect(n3_sb[:]), in1=g[:], op=ALU.mult)
             return lambda: nc.scalar.activation(out=h2[u][:].indirect(n3_sb[:]), in_=ra[:], func=ACT.Copy)
 
-        def scatter_on_vector(u):
+        def scatter_on_vector(u, engine):
             old = sb.tile([P, U], F32, name="old%d" % u)
-            nc.vector.tensor_copy(out=old[:], in_=h2[u][:].indirect(n3_sb[:]))
+            gather(nc, engine, old[:], h2[u][:], n3_sb[:])
             return lambda g: nc.vector.tensor_tensor(out=h2[u][:].indirect(n3_sb[:]), in0=old[:], in1=g[:], op=ALU.mult)
 
-        nc.vector.tensor_copy(out=h2[0][:, :S], in_=h2_ps[0][:])
+        nc.scalar.copy(out=h2[0][:, halves[0]], in_=early[0][0][:])
+        nc.scalar.copy(out=h2[1][:, halves[0]], in_=early[1][0][:])
+        nc.vector.tensor_copy(out=h2[0][:, halves[1]], in_=early[0][1][:])
+        nc.vector.tensor_copy(out=h2[1][:, halves[1]], in_=early[1][1][:])
         gate0 = gate(0)
-        nc.vector.tensor_copy(out=h2[1][:, :S], in_=h2_ps[1][:])
-        nc.scalar.copy(out=h2[2][:, :S], in_=h2_ps[2][:])
-        put1 = scatter_on_vector(1)
-        gate2 = gate(2)
-        put0 = scatter_on_scalar(0, gate0)
+        nc.vector.tensor_copy(out=h2[2][:, :S], in_=late[0][:])
+        nc.vector.tensor_copy(out=h2[3][:, :S], in_=late[1][:])
         gate1 = gate(1)
-        put2 = scatter_on_scalar(2, gate2)
+        put0 = scatter_on_scalar(0, gate0)
+        gate2 = gate(2)
+        put1 = scatter_on_scalar(1, gate1)
+        put2 = scatter_on_vector(2, "scalar")
+        gate3 = gate(3)
+        put3 = scatter_on_vector(3, "vector")
         put0()
         store(0)
-        put1(gate1)
-        store(1)
-        nc.scalar.copy(out=h2[3][:, :S], in_=h2_ps[3][:])
-        gate3 = gate(3)
-        put3 = scatter_on_vector(3)
-        put2()
+        put2(gate2)
         store(2)
+        put1()
+        store(1)
         put3(gate3)
         store(3)

@@ -17,18 +17,41 @@ PACK = 4
 T = 2048
 S = 512
 U = 384
-FLOPS = 2 * 2 * 512 * 512 * 512
+GROUP = 16
+FLOPS = 2 * 2 * S * S * S
 
-H_WINDOW = 520
-ST_WINDOW = 688
-H2_WINDOW = 768
+H_WINDOW = S + 8
+
+ALL = slice(0, S)
+HALVES = [slice(0, S // 2), slice(S // 2, S)]
 
 
-def gather(nc, engine, out, window, offsets):
-    if engine == "vector":
-        nc.vector.tensor_copy(out=out, in_=window.indirect(offsets))
-    else:
-        nc.scalar.activation(out=out, in_=window.indirect(offsets), func=ACT.Copy)
+def entries(offsets, part):
+    return offsets[:, part.start // GROUP : part.stop // GROUP]
+
+
+def gather_shared(nc, engines, out, window, offsets):
+    n = out.shape[1] // len(engines)
+    for i, engine in enumerate(engines):
+        part = slice(n * i, n * (i + 1))
+        picked = window[:].indirect(entries(offsets, part))
+        if engine == "vector":
+            nc.vector.tensor_copy(out=out[:, part], in_=picked)
+        else:
+            nc.scalar.activation(out=out[:, part], in_=picked, func=ACT.Copy)
+
+
+def product(nc, dst, lhs_codes, lhs_scales, block, rhs_codes, rhs_scales, cols):
+    rows = slice(P * block, P * (block + 1))
+    nc.tensor.matmul_mx(
+        out=dst,
+        lhsT=lhs_codes[:, rows].bitcast(FP8X4),
+        lhsT_scale=lhs_scales[:, rows],
+        rhs=rhs_codes[:, cols].bitcast(FP8X4),
+        rhs_scale=rhs_scales[:, cols],
+        start=True,
+        stop=True,
+    )
 
 
 def tile_picked_hpqghopmkgate_none_p_kernel(
@@ -45,21 +68,20 @@ def tile_picked_hpqghopmkgate_none_p_kernel(
             nc.sync.dma_start(out=dst[:], in_=src)
             return dst
 
-        def load_scale_table(src, name, memset_engine):
+        def load_scale_table(src, name):
             dst = sb.tile([P, T], U8, name=name, tag=name, align_bytes=64)
-            memset_engine.memset(dst[:].bitcast(I32), 0)
-            nc.sync.dma_start(out=dst[0:P:8, :].bitcast(I32), in_=src[0].bitcast(I32))
+            nc.sync.dma_start(out=dst[:].bitcast(I32), in_=src[0].bitcast(I32).unsqueeze(1).to_broadcast([16, 8, T // 4]))
             return dst
 
         def load_word_table(src, name):
             dst = sb.tile([P, T], I32, name=name, tag=name, align_bytes=64)
-            nc.sync.dma_start(out=dst[:], in_=src[0].rearrange("p n t -> p (n t)").bitcast(I32))
+            nc.sync.dma_start(out=dst[:], in_=src[0].rearrange("p n r -> p (n r)").bitcast(I32))
             return dst
 
         k1_sb = load_list(k1, "k1_sb")
+        d_scale_table = load_scale_table(d_scales, "d_scale_table")
         offs_sb = load_list(offs, "offs_sb")
-        d_scale_table = load_scale_table(d_scales, "d_scale_table", nc.gpsimd)
-        x_scale_table = load_scale_table(x_scales, "x_scale_table", nc.vector)
+        x_scale_table = load_scale_table(x_scales, "x_scale_table")
         d_word_table = load_word_table(d_words, "d_word_table")
         x_word_table = load_word_table(x_words, "x_word_table")
         n1_sb = load_list(n1, "n1_sb")
@@ -68,9 +90,9 @@ def tile_picked_hpqghopmkgate_none_p_kernel(
         n4_sb = load_list(n4, "n4_sb")
 
         h = [sb.tile([P, H_WINDOW], F32, name="h%d" % t) for t in range(PACK)]
-        st = [sb.tile([P, ST_WINDOW], F32, name="st%d" % t) for t in range(PACK)]
-        h2 = [sb.tile([P, H2_WINDOW], F32, name="h2_%d" % t) for t in range(PACK)]
-        for window in h + st + h2:
+        st = [sb.tile([P, S], F32, name="st%d" % t) for t in range(PACK)]
+        h2 = [sb.tile([P, S], F32, name="h2_%d" % u) for u in range(PACK)]
+        for window in h:
             nc.gpsimd.memset(window[:, S:], 0.0)
 
         warm = sb.tile([P, 1], F32, name="warm")
@@ -88,36 +110,31 @@ def tile_picked_hpqghopmkgate_none_p_kernel(
         for j in range(1, 4):
             nc.scalar.dma_start(out=planes[j:P:32, :].bitcast(I32), in_=planes[8 * j : P : 32, :].bitcast(I32))
 
-        halves = [slice(0, S // 2), slice(S // 2, S)]
         w_rows = w1.rearrange("(p t) m -> p t m", t=PACK)
         w_raw0 = sb.tile([P, PACK, S // 2], F32, name="w_raw0", tag="x_bytes", align_bytes=64)
-        nc.scalar.dma_start(out=w_raw0[:], in_=w_rows[:, :, halves[0]])
+        nc.scalar.dma_start(out=w_raw0[:], in_=w_rows[:, :, HALVES[0]])
 
         gn_sb = sb.tile([P, PACK], F32, name="gn_sb", tag="d_bytes", align_bytes=64)
         nc.sync.dma_start(out=gn_sb[:], in_=gn.rearrange("(p t) o -> p (t o)", t=PACK))
 
         d_picked = sb.tile([P, S], I32, name="d_picked", align_bytes=64)
-        for c in halves:
-            nc.vector.tensor_copy(
-                out=d_picked[:, c].bitcast(U32), in_=d_word_table[:].bitcast(U32).indirect(k1_sb[:, c.start // 16 : c.stop // 16])
-            )
+        for c in HALVES:
+            nc.vector.tensor_copy(out=d_picked[:, c].bitcast(U32), in_=d_word_table[:].bitcast(U32).indirect(entries(k1_sb, c)))
         d_dealt = sb.tile([P, S], I32, name="d_dealt", align_bytes=64)
-        for c in halves:
+        for c in HALVES:
             nc.vector.tensor_copy(
                 out=d_dealt[:].rearrange("p (t a i) -> p a t i", t=PACK, i=4)[:, c.start // 16 : c.stop // 16],
                 in_=d_picked[:, c].rearrange("p (a i t) -> p a t i", t=PACK, i=4),
             )
         x_picked = sb.tile([P, S], I32, name="x_picked", align_bytes=64)
-        for c in halves:
-            nc.vector.tensor_copy(
-                out=x_picked[:, c].bitcast(U32), in_=x_word_table[:].bitcast(U32).indirect(offs_sb[:, c.start // 16 : c.stop // 16])
-            )
+        for c in HALVES:
+            nc.vector.tensor_copy(out=x_picked[:, c].bitcast(U32), in_=x_word_table[:].bitcast(U32).indirect(entries(offs_sb, c)))
 
         w_raw1 = sb.tile([P, PACK, S // 2], F32, name="w_raw1", tag="x_word_table", align_bytes=64)
-        nc.sync.dma_start(out=w_raw1[:], in_=w_rows[:, :, halves[1]])
+        nc.sync.dma_start(out=w_raw1[:], in_=w_rows[:, :, HALVES[1]])
 
         def quantize_w(raw, copy, grouped_tag, codes_tag):
-            w_grouped = sb.tile([P, 256 * PACK], BF16, name="w_grouped", tag=grouped_tag, align_bytes=64)
+            w_grouped = sb.tile([P, S // 2 * PACK], BF16, name="w_grouped", tag=grouped_tag, align_bytes=64)
             copy(
                 out=w_grouped[:].rearrange("p (c i t) -> p c t i", t=PACK, i=4),
                 in_=raw[:].rearrange("p t (c i) -> p c t i", i=4),
@@ -127,61 +144,45 @@ def tile_picked_hpqghopmkgate_none_p_kernel(
             nc.vector.quantize_mx(out=codes[:].bitcast(FP8X4), scales=scales[:], in_=w_grouped[:])
             return codes, scales
 
-        def product(dst, lhs_codes, lhs_scales, t, rhs_codes, rhs_scales, c):
-            rows = slice(P * t, P * (t + 1))
-            nc.tensor.matmul_mx(
-                out=dst,
-                lhsT=lhs_codes[:, rows].bitcast(FP8X4),
-                lhsT_scale=lhs_scales[:, rows],
-                rhs=rhs_codes[:, c].bitcast(FP8X4),
-                rhs_scale=rhs_scales[:, c],
-                start=True,
-                stop=True,
-            )
-
         h_ps = [psum.tile([P, S], F32, name="h_ps%d" % t, tag="bank%d" % t) for t in range(PACK)]
         for t in range(PACK):
-            for c in halves if t == 0 else [slice(0, S)]:
-                product(h_ps[t][:, c], d_dealt, planes[:, S:], t, x_picked, planes[:, :S], c)
+            for c in HALVES if t == 0 else [ALL]:
+                product(nc, h_ps[t][:, c], d_dealt, planes[:, S:], t, x_picked, planes[:, :S], c)
         w_codes0, w_scales0 = quantize_w(w_raw0, nc.vector.tensor_copy, "w_grouped0", "w_codes0")
 
-        members = [sb.tile([P, 2 * S], F32, name="members%d" % t, tag="members%d" % t, align_bytes=64) for t in range(PACK)]
-        z_both = [sb.tile([P, 2 * S], BF16, name="z_both%d" % i, align_bytes=64) for i in range(2)]
-        z_pairs = [[z_both[i][:, S * e : S * (e + 1)] for e in range(2)] for i in range(2)]
+        members = [sb.tile([P, 2 * S], F32, name="members%d" % t, align_bytes=64) for t in range(PACK)]
+        other = [sb.tile([P, S], F32, name="other%d" % t) for t in range(PACK)]
+        z_pairs = [sb.tile([P, 2 * S], BF16, name="z_pairs%d" % i, align_bytes=64) for i in range(2)]
 
         def leave_psum(t):
             nc.scalar.activation(out=h[t][:, :S], in_=h_ps[t][:], func=ACT.Copy, scale=0.0625)
 
         def fetch_members(t, engine):
-            for half in range(2):
-                gather(nc, engine, members[t][:, S * half : S * (half + 1)], h[t][:], n1_sb[:, 32 * half : 32 * (half + 1)])
+            gather_shared(nc, [engine, engine], members[t], h[t], n1_sb)
 
         def make_st(t):
             mx = sb.tile([P, S], F32, name="mx%d" % t, tag="mx%d" % t, align_bytes=64)
-            for c in halves:
+            for c in HALVES:
                 nc.vector.tensor_tensor(
                     out=mx[:, c],
                     in0=members[t][:, 2 * c.start : 2 * c.stop : 2],
                     in1=members[t][:, 2 * c.start + 1 : 2 * c.stop : 2],
                     op=ALU.max,
                 )
-            for c in halves:
+            for c in HALVES:
                 nc.vector.tensor_tensor(out=st[t][:, c], in0=h[t][:, c], in1=mx[:, c], op=ALU.subtract)
 
-        other = [sb.tile([P, S], F32, name="other%d" % t) for t in range(PACK)]
-
-        def fetch_other(t, *engines):
-            n = S // len(engines)
-            for i, engine in enumerate(engines):
-                gather(nc, engine, other[t][:, n * i : n * (i + 1)], st[t][:], n2_sb[:, n * i // 16 : n * (i + 1) // 16])
+        def fetch_other(t, engine):
+            gather_shared(nc, [engine, engine], other[t], st[t], n2_sb)
 
         def make_z(t):
             larger = sb.tile([P, S], F32, name="larger%d" % t)
-            for c in halves:
+            for c in HALVES:
                 nc.vector.tensor_tensor(out=larger[:, c], in0=st[t][:, c], in1=other[t][:, c], op=ALU.max)
-            for i, c in enumerate(halves):
+            for i, c in enumerate(HALVES):
+                pair = z_pairs[i][:, S * (t // 2) : S * (t // 2 + 1)]
                 nc.vector.tensor_scalar(
-                    out=z_pairs[i][t // 2][:, t % 2 : S : 2], in0=larger[:, c], scalar1=gn_sb[:, t : t + 1], scalar2=None, op0=ALU.mult
+                    out=pair[:, t % 2 : S : 2], in0=larger[:, c], scalar1=gn_sb[:, t : t + 1], scalar2=None, op0=ALU.mult
                 )
 
         leave_psum(0)
@@ -193,75 +194,77 @@ def tile_picked_hpqghopmkgate_none_p_kernel(
         leave_psum(3)
         fetch_members(2, "scalar")
         make_st(1)
-        fetch_other(0, "vector", "vector")
+        fetch_other(0, "vector")
         make_z(0)
         fetch_members(3, "scalar")
         make_st(2)
-        fetch_other(1, "scalar", "scalar")
+        fetch_other(1, "scalar")
         make_st(3)
         make_z(1)
-        fetch_other(2, "scalar", "scalar")
-        fetch_other(3, "scalar", "scalar")
+        fetch_other(2, "scalar")
+        fetch_other(3, "scalar")
         make_z(2)
         make_z(3)
 
         z_codes = sb.tile([P, S], I32, name="z_codes", align_bytes=64)
         z_scales = sb.tile([P, S], U8, name="z_scales", align_bytes=64)
-        z_grouped = [sb.tile([P, S * 2], BF16, name="z_grouped%d" % i, tag="z_grouped%d" % i, align_bytes=64) for i in range(2)]
+        z_grouped = [sb.tile([P, 2 * S], BF16, name="z_grouped%d" % i, tag="z_grouped%d" % i, align_bytes=64) for i in range(2)]
         for i in range(2):
             nc.vector.tensor_copy(
                 out=z_grouped[i][:].bitcast(I32).rearrange("p (c e) -> p c e", e=2),
-                in_=z_both[i][:].bitcast(I32).rearrange("p (e c) -> p c e", e=2),
+                in_=z_pairs[i][:].bitcast(I32).rearrange("p (e c) -> p c e", e=2),
             )
-        for i, c in enumerate(halves):
+        for i, c in enumerate(HALVES):
             nc.vector.quantize_mx(out=z_codes[:, c].bitcast(FP8X4), scales=z_scales[:, c], in_=z_grouped[i][:])
         w_codes1, w_scales1 = quantize_w(w_raw1, nc.scalar.copy, "mx3", "z_grouped1")
 
-        early = [[psum.tile([P, S // 2], F32, name="early%d%d" % (u, i), tag="bank%d" % (4 + 2 * u + i)) for i in range(2)] for u in range(2)]
+        early = [
+            [psum.tile([P, S // 2], F32, name="early%d%d" % (u, i), tag="bank%d" % (PACK + 2 * u + i)) for i in range(2)]
+            for u in range(2)
+        ]
         late = [psum.tile([P, S], F32, name="late%d" % u, tag="bank%d" % u) for u in range(2)]
-        for i, c in enumerate(halves):
+        for i, c in enumerate(HALVES):
             for u in range(2):
-                product(early[u][i][:], w_codes0, w_scales0, u, z_codes, z_scales, c)
+                product(nc, early[u][i][:], w_codes0, w_scales0, u, z_codes, z_scales, c)
         for u in range(2):
-            product(late[u][:], w_codes1, w_scales1, u, z_codes, z_scales, slice(0, S))
+            product(nc, late[u][:], w_codes1, w_scales1, u, z_codes, z_scales, ALL)
 
         def gate(u):
             g = sb.tile([P, U], F32, name="gate%d" % u)
-            nc.scalar.activation(out=g[:], in_=h2[u][:].indirect(n4_sb[:]), func=ACT.Sigmoid)
+            for part in (slice(0, U // 2), slice(U // 2, U)):
+                nc.scalar.activation(out=g[:, part], in_=h2[u][:].indirect(entries(n4_sb, part)), func=ACT.Sigmoid)
             return g
 
-        def store(u):
-            nc.sync.dma_start(out=out[P * u : P * (u + 1), :], in_=h2[u][:, :S])
-
-        def scatter_on_scalar(u, g):
+        def gated(u, g):
             ra = sb.tile([P, U], F32, name="ra%d" % u)
             nc.vector.tensor_tensor(out=ra[:], in0=h2[u][:].indirect(n3_sb[:]), in1=g[:], op=ALU.mult)
-            return lambda: nc.scalar.activation(out=h2[u][:].indirect(n3_sb[:]), in_=ra[:], func=ACT.Copy)
+            return ra
 
-        def scatter_on_vector(u, engine):
+        def old_values(u, engines):
             old = sb.tile([P, U], F32, name="old%d" % u)
-            gather(nc, engine, old[:], h2[u][:], n3_sb[:])
-            return lambda g: nc.vector.tensor_tensor(out=h2[u][:].indirect(n3_sb[:]), in0=old[:], in1=g[:], op=ALU.mult)
+            gather_shared(nc, engines, old, h2[u], n3_sb)
+            return old
 
-        nc.scalar.copy(out=h2[0][:, halves[0]], in_=early[0][0][:])
-        nc.scalar.copy(out=h2[1][:, halves[0]], in_=early[1][0][:])
-        nc.vector.tensor_copy(out=h2[0][:, halves[1]], in_=early[0][1][:])
-        nc.vector.tensor_copy(out=h2[1][:, halves[1]], in_=early[1][1][:])
+        def store(u):
+            nc.sync.dma_start(out=out[P * u : P * (u + 1), :], in_=h2[u][:])
+
+        for u in range(2):
+            nc.scalar.copy(out=h2[u][:, HALVES[0]], in_=early[u][0][:])
+        for u in range(2):
+            nc.vector.tensor_copy(out=h2[u][:, HALVES[1]], in_=early[u][1][:])
         gate0 = gate(0)
-        nc.vector.tensor_copy(out=h2[2][:, :S], in_=late[0][:])
-        nc.vector.tensor_copy(out=h2[3][:, :S], in_=late[1][:])
+        for u in range(2):
+            nc.vector.tensor_copy(out=h2[2 + u][:], in_=late[u][:])
         gate1 = gate(1)
-        put0 = scatter_on_scalar(0, gate0)
+        ra0 = gated(0, gate0)
         gate2 = gate(2)
-        put1 = scatter_on_scalar(1, gate1)
-        put2 = scatter_on_vector(2, "scalar")
+        ra1 = gated(1, gate1)
+        old2 = old_values(2, ["scalar", "vector"])
         gate3 = gate(3)
-        put3 = scatter_on_vector(3, "vector")
-        put0()
-        store(0)
-        put2(gate2)
-        store(2)
-        put1()
-        store(1)
-        put3(gate3)
-        store(3)
+        old3 = old_values(3, ["vector"])
+
+        for u, ra, old, g in ((0, ra0, old2, gate2), (1, ra1, old3, gate3)):
+            nc.scalar.activation(out=h2[u][:].indirect(n3_sb[:]), in_=ra[:], func=ACT.Copy)
+            store(u)
+            nc.vector.tensor_tensor(out=h2[2 + u][:].indirect(n3_sb[:]), in0=old[:], in1=g[:], op=ALU.mult)
+            store(2 + u)

@@ -70,7 +70,8 @@ def tile_picked_hpqghopmkgate_none_p_kernel(
 
         def load_scale_table(src, name):
             dst = sb.tile([P, T], U8, name=name, tag=name, align_bytes=64)
-            nc.sync.dma_start(out=dst[:].bitcast(I32), in_=src[0].bitcast(I32).unsqueeze(1).to_broadcast([16, 8, T // 4]))
+            nc.vector.memset(dst[:].bitcast(I32), 0)
+            nc.sync.dma_start(out=dst[0:P:8, :].bitcast(I32), in_=src[0].bitcast(I32))
             return dst
 
         def load_word_table(src, name):
@@ -79,8 +80,8 @@ def tile_picked_hpqghopmkgate_none_p_kernel(
             return dst
 
         k1_sb = load_list(k1, "k1_sb")
-        d_scale_table = load_scale_table(d_scales, "d_scale_table")
         offs_sb = load_list(offs, "offs_sb")
+        d_scale_table = load_scale_table(d_scales, "d_scale_table")
         x_scale_table = load_scale_table(x_scales, "x_scale_table")
         d_word_table = load_word_table(d_words, "d_word_table")
         x_word_table = load_word_table(x_words, "x_word_table")
@@ -93,7 +94,7 @@ def tile_picked_hpqghopmkgate_none_p_kernel(
         st = [sb.tile([P, S], F32, name="st%d" % t) for t in range(PACK)]
         h2 = [sb.tile([P, S], F32, name="h2_%d" % u) for u in range(PACK)]
         for window in h:
-            nc.gpsimd.memset(window[:, S:], 0.0)
+            nc.vector.memset(window[:, S:], 0.0)
 
         warm = sb.tile([P, 1], F32, name="warm")
         nc.scalar.activation(out=warm[:], in_=h[0][:, S : S + 1], func=ACT.Sigmoid)

from contextlib import ExitStack

import concourse.mybir as mybir

F32 = mybir.dt.float32
BF16 = mybir.dt.bfloat16
I32 = mybir.dt.int32
U32 = mybir.dt.uint32
U16 = mybir.dt.uint16
U8 = mybir.dt.uint8
FP8X4 = mybir.dt.float8_e4m3fn_x4
ALU = mybir.AluOpType
ACT = mybir.ActivationFunctionType

P = 128
PACK = 4
T = 2048
S = 512
U = 384
GROUP = 16
FLOPS = 2 * 2 * S * S * S

H_WINDOW = S + 8

ALL = slice(0, S)
HALVES = [slice(0, S // 2), slice(S // 2, S)]


def entries(offsets, part):
    return offsets[:, part.start // GROUP : part.stop // GROUP]


def gather_shared(nc, engines, out, window, offsets):
    n = out.shape[1] // len(engines)
    for i, engine in enumerate(engines):
        part = slice(n * i, n * (i + 1))
        picked = window[:].indirect(entries(offsets, part))
        if engine == "vector":
            nc.vector.tensor_copy(out=out[:, part], in_=picked)
        else:
            nc.scalar.activation(out=out[:, part], in_=picked, func=ACT.Copy)


def product(nc, dst, lhs_codes, lhs_scales, block, rhs_codes, rhs_scales, cols):
    rows = slice(P * block, P * (block + 1))
    nc.tensor.matmul_mx(
        out=dst,
        lhsT=lhs_codes[:, rows].bitcast(FP8X4),
        lhsT_scale=lhs_scales[:, rows],
        rhs=rhs_codes[:, cols].bitcast(FP8X4),
        rhs_scale=rhs_scales[:, cols],
        start=True,
        stop=True,
    )


def tile_picked_hpqghopmkgate_none_p_kernel(
    tc, x_words, x_scales, d_words, d_scales, gn, w1, offs, k1, n1, n2, n3, n4, out
):
    nc = tc.nc
    with ExitStack() as ctx:
        lists = ctx.enter_context(tc.tile_pool(name="lists", bufs=1))
        sb = ctx.enter_context(tc.tile_pool(name="sb", bufs=1))
        psum = ctx.enter_context(tc.psum_pool(name="psum", bufs=1))

        def load_list(src, name):
            dst = lists.tile(list(src.shape), U16, name=name)
            nc.sync.dma_start(out=dst[:], in_=src)
            return dst

        def load_scale_table(src, name):
            dst = sb.tile([P, T], U8, name=name, tag=name, align_bytes=64)
            nc.vector.memset(dst[:].bitcast(I32), 0)
            nc.sync.dma_start(out=dst[0:P:8, :].bitcast(I32), in_=src[0].bitcast(I32))
            return dst

        def load_word_table(src, name):
            dst = sb.tile([P, T], I32, name=name, tag=name, align_bytes=64)
            nc.sync.dma_start(out=dst[:], in_=src[0].rearrange("p n r -> p (n r)").bitcast(I32))
            return dst

        k1_sb = load_list(k1, "k1_sb")
        offs_sb = load_list(offs, "offs_sb")
        d_scale_table = load_scale_table(d_scales, "d_scale_table")
        x_scale_table = load_scale_table(x_scales, "x_scale_table")
        d_word_table = load_word_table(d_words, "d_word_table")
        x_word_table = load_word_table(x_words, "x_word_table")
        n1_sb = load_list(n1, "n1_sb")
        n2_sb = load_list(n2, "n2_sb")
        n3_sb = load_list(n3, "n3_sb")
        n4_sb = load_list(n4, "n4_sb")

        h = [sb.tile([P, H_WINDOW], F32, name="h%d" % t) for t in range(PACK)]
        st = [sb.tile([P, S], F32, name="st%d" % t) for t in range(PACK)]
        h2 = [sb.tile([P, S], F32, name="h2_%d" % u) for u in range(PACK)]
        for window in h:
            nc.vector.memset(window[:, S:], 0.0)

        warm = sb.tile([P, 1], F32, name="warm")
        nc.scalar.activation(out=warm[:], in_=h[0][:, S : S + 1], func=ACT.Sigmoid)

        d_bytes = sb.tile([P, S], U8, name="d_bytes", tag="d_bytes", align_bytes=64)
        nc.vector.tensor_copy(out=d_bytes[:], in_=d_scale_table[:].indirect(k1_sb[:]))
        x_bytes = sb.tile([P, S], U8, name="x_bytes", tag="x_bytes", align_bytes=64)
        nc.vector.tensor_copy(out=x_bytes[:], in_=x_scale_table[:].indirect(offs_sb[:]))
        planes = sb.tile([P, 2 * S], U8, name="planes", tag="x_scale_table", align_bytes=64)
        nc.vector.tensor_copy(
            out=planes[:, S:].rearrange("p (t m) -> p t m", t=PACK), in_=d_bytes[:].rearrange("p (m t) -> p t m", t=PACK)
        )
        nc.vector.tensor_copy(out=planes[:, :S].bitcast(I32), in_=x_bytes[:].bitcast(I32))
        for j in range(1, 4):
            nc.scalar.dma_start(out=planes[j:P:32, :].bitcast(I32), in_=planes[8 * j : P : 32, :].bitcast(I32))

        w_rows = w1.rearrange("(p t) m -> p t m", t=PACK)
        w_raw0 = sb.tile([P, PACK, S // 2], F32, name="w_raw0", tag="x_bytes", align_bytes=64)
        nc.scalar.dma_start(out=w_raw0[:], in_=w_rows[:, :, HALVES[0]])

        gn_sb = sb.tile([P, PACK], F32, name="gn_sb", tag="d_bytes", align_bytes=64)
        nc.sync.dma_start(out=gn_sb[:], in_=gn.rearrange("(p t) o -> p (t o)", t=PACK))

        d_picked = sb.tile([P, S], I32, name="d_picked", align_bytes=64)
        for c in HALVES:
            nc.vector.tensor_copy(out=d_picked[:, c].bitcast(U32), in_=d_word_table[:].bitcast(U32).indirect(entries(k1_sb, c)))
        d_dealt = sb.tile([P, S], I32, name="d_dealt", align_bytes=64)
        for c in HALVES:
            nc.vector.tensor_copy(
                out=d_dealt[:].rearrange("p (t a i) -> p a t i", t=PACK, i=4)[:, c.start // 16 : c.stop // 16],
                in_=d_picked[:, c].rearrange("p (a i t) -> p a t i", t=PACK, i=4),
            )
        x_picked = sb.tile([P, S], I32, name="x_picked", align_bytes=64)
        for c in HALVES:
            nc.vector.tensor_copy(out=x_picked[:, c].bitcast(U32), in_=x_word_table[:].bitcast(U32).indirect(entries(offs_sb, c)))

        w_raw1 = sb.tile([P, PACK, S // 2], F32, name="w_raw1", tag="x_word_table", align_bytes=64)
        nc.sync.dma_start(out=w_raw1[:], in_=w_rows[:, :, HALVES[1]])

        def quantize_w(raw, copy, grouped_tag, codes_tag):
            w_grouped = sb.tile([P, S // 2 * PACK], BF16, name="w_grouped", tag=grouped_tag, align_bytes=64)
            copy(
                out=w_grouped[:].rearrange("p (c i t) -> p c t i", t=PACK, i=4),
                in_=raw[:].rearrange("p t (c i) -> p c t i", i=4),
            )
            codes = sb.tile([P, S // 2], I32, name="w_codes", tag=codes_tag, align_bytes=64)
            scales = sb.tile([P, S // 2], U8, name="w_scales", tag=codes_tag + "_scales", align_bytes=64)
            nc.vector.quantize_mx(out=codes[:].bitcast(FP8X4), scales=scales[:], in_=w_grouped[:])
            return codes, scales

        h_ps = [psum.tile([P, S], F32, name="h_ps%d" % t, tag="bank%d" % t) for t in range(PACK)]
        for t in range(PACK):
            for c in HALVES if t == 0 else [ALL]:
                product(nc, h_ps[t][:, c], d_dealt, planes[:, S:], t, x_picked, planes[:, :S], c)
        w_codes0, w_scales0 = quantize_w(w_raw0, nc.vector.tensor_copy, "w_grouped0", "w_codes0")

        members = [sb.tile([P, 2 * S], F32, name="members%d" % t, align_bytes=64) for t in range(PACK)]
        other = [sb.tile([P, S], F32, name="other%d" % t) for t in range(PACK)]
        z_pairs = [sb.tile([P, 2 * S], BF16, name="z_pairs%d" % i, align_bytes=64) for i in range(2)]

        def leave_psum(t):
            nc.scalar.activation(out=h[t][:, :S], in_=h_ps[t][:], func=ACT.Copy, scale=0.0625)

        def fetch_members(t, engine):
            gather_shared(nc, [engine, engine], members[t], h[t], n1_sb)

        def make_st(t):
            mx = sb.tile([P, S], F32, name="mx%d" % t, tag="mx%d" % t, align_bytes=64)
            for c in HALVES:
                nc.vector.tensor_tensor(
                    out=mx[:, c],
                    in0=members[t][:, 2 * c.start : 2 * c.stop : 2],
                    in1=members[t][:, 2 * c.start + 1 : 2 * c.stop : 2],
                    op=ALU.max,
                )
            for c in HALVES:
                nc.vector.tensor_tensor(out=st[t][:, c], in0=h[t][:, c], in1=mx[:, c], op=ALU.subtract)

        def fetch_other(t, engine):
            gather_shared(nc, [engine, engine], other[t], st[t], n2_sb)

        def make_z(t):
            larger = sb.tile([P, S], F32, name="larger%d" % t)
            for c in HALVES:
                nc.vector.tensor_tensor(out=larger[:, c], in0=st[t][:, c], in1=other[t][:, c], op=ALU.max)
            for i, c in enumerate(HALVES):
                pair = z_pairs[i][:, S * (t // 2) : S * (t // 2 + 1)]
                nc.vector.tensor_scalar(
                    out=pair[:, t % 2 : S : 2], in0=larger[:, c], scalar1=gn_sb[:, t : t + 1], scalar2=None, op0=ALU.mult
                )

        leave_psum(0)
        leave_psum(1)
        leave_psum(2)
        fetch_members(0, "vector")
        fetch_members(1, "scalar")
        make_st(0)
        leave_psum(3)
        fetch_members(2, "scalar")
        make_st(1)
        fetch_other(0, "vector")
        make_z(0)
        fetch_members(3, "scalar")
        make_st(2)
        fetch_other(1, "scalar")
        make_st(3)
        make_z(1)
        fetch_other(2, "scalar")
        fetch_other(3, "scalar")
        make_z(2)
        make_z(3)

        z_codes = sb.tile([P, S], I32, name="z_codes", align_bytes=64)
        z_scales = sb.tile([P, S], U8, name="z_scales", align_bytes=64)
        z_grouped = [sb.tile([P, 2 * S], BF16, name="z_grouped%d" % i, tag="z_grouped%d" % i, align_bytes=64) for i in range(2)]
        for i in range(2):
            nc.vector.tensor_copy(
                out=z_grouped[i][:].bitcast(I32).rearrange("p (c e) -> p c e", e=2),
                in_=z_pairs[i][:].bitcast(I32).rearrange("p (e c) -> p c e", e=2),
            )
        for i, c in enumerate(HALVES):
            nc.vector.quantize_mx(out=z_codes[:, c].bitcast(FP8X4), scales=z_scales[:, c], in_=z_grouped[i][:])
        w_codes1, w_scales1 = quantize_w(w_raw1, nc.scalar.copy, "mx3", "z_grouped1")

        early = [
            [psum.tile([P, S // 2], F32, name="early%d%d" % (u, i), tag="bank%d" % (PACK + 2 * u + i)) for i in range(2)]
            for u in range(2)
        ]
        late = [psum.tile([P, S], F32, name="late%d" % u, tag="bank%d" % u) for u in range(2)]
        for i, c in enumerate(HALVES):
            for u in range(2):
                product(nc, early[u][i][:], w_codes0, w_scales0, u, z_codes, z_scales, c)
        for u in range(2):
            product(nc, late[u][:], w_codes1, w_scales1, u, z_codes, z_scales, ALL)

        def gate(u):
            g = sb.tile([P, U], F32, name="gate%d" % u)
            for part in (slice(0, U // 2), slice(U // 2, U)):
                nc.scalar.activation(out=g[:, part], in_=h2[u][:].indirect(entries(n4_sb, part)), func=ACT.Sigmoid)
            return g

        def gated(u, g):
            ra = sb.tile([P, U], F32, name="ra%d" % u)
            nc.vector.tensor_tensor(out=ra[:], in0=h2[u][:].indirect(n3_sb[:]), in1=g[:], op=ALU.mult)
            return ra

        def old_values(u, engines):
            old = sb.tile([P, U], F32, name="old%d" % u)
            gather_shared(nc, engines, old, h2[u], n3_sb)
            return old

        def store(u):
            nc.sync.dma_start(out=out[P * u : P * (u + 1), :], in_=h2[u][:])

        for u in range(2):
            nc.scalar.copy(out=h2[u][:, HALVES[0]], in_=early[u][0][:])
        for u in range(2):
            nc.vector.tensor_copy(out=h2[u][:, HALVES[1]], in_=early[u][1][:])
        gate0 = gate(0)
        for u in range(2):
            nc.vector.tensor_copy(out=h2[2 + u][:], in_=late[u][:])
        gate1 = gate(1)
        ra0 = gated(0, gate0)
        gate2 = gate(2)
        ra1 = gated(1, gate1)
        old2 = old_values(2, ["scalar", "vector"])
        gate3 = gate(3)
        old3 = old_values(3, ["vector"])

        for u, ra, old, g in ((0, ra0, old2, gate2), (1, ra1, old3, gate3)):
            nc.scalar.activation(out=h2[u][:].indirect(n3_sb[:]), in_=ra[:], func=ACT.Copy)
            store(u)
            nc.vector.tensor_tensor(out=h2[2 + u][:].indirect(n3_sb[:]), in0=old[:], in1=g[:], op=ALU.mult)
            store(2 + u)
